import numpy as np
import ml_dtypes


def mxq(x, axis, fmt="e4m3"):
    dtype, down = {"e4m3": (ml_dtypes.float8_e4m3fn, 7), "e5m2": (ml_dtypes.float8_e5m2, 14)}[fmt]
    v = np.moveaxis(np.asarray(x, np.float32).astype(ml_dtypes.bfloat16).astype(np.float64), axis, -1)
    blocks = v.reshape(v.shape[:-1] + (-1, 32))
    amax = np.abs(blocks).max(-1, keepdims=True)
    byte = np.maximum(np.where(amax > 0, np.frexp(amax)[1] - 1 + 127, 0) - down, 1)
    scale = np.exp2(byte - 127.0)
    codes = (blocks / scale).astype(np.float32).astype(dtype).astype(np.float64)
    return np.moveaxis((codes * scale).reshape(v.shape), -1, axis)


WIDE = False


def mx_kscale(k):
    if not WIDE:
        return np.ones(k)
    levels = np.array([30, -30])
    if k % 512:
        return np.exp2(np.random.permutation(np.resize(levels, k // 32))).repeat(32)
    a = np.empty((k // 512, 16))
    for p in range(k // 512):
        a[p, :8] = np.random.permutation(np.resize(levels, 8))
        for g in range(8):
            far = levels[np.abs(levels - a[p, g]) >= 10]
            a[p, g + 8] = far[np.random.randint(len(far))]
    return np.exp2(a.ravel()).repeat(32)


def f64(x):
    return np.asarray(x).astype(np.float64)


K, L, M, T = 1024, 1024, 512, 512


def setup_inputs():
    n = np.random.standard_normal
    s1 = mx_kscale(K)[:, None]
    s2 = mx_kscale(L)[:, None]
    m = np.exp(0.5 * n((1, T)))
    return {
        "w": (n((K, M)) / np.sqrt(K) / s1).astype(np.float32),
        "dy": (m * n((K, T)) * s1).astype(np.float32),
        "v": (n((L, M)) / np.sqrt(L) / s2).astype(np.float32),
        "e": (n((L, T)) * s2).astype(np.float32),
        "r": (n((512, 512))).astype(np.float32),
    }


def reference(w, dy, v, e, r):
    w_ = mxq(f64(w), 0, "e4m3")
    dy_ = mxq(f64(dy), 0, "e5m2")
    v_ = mxq(f64(v), 0, "e4m3")
    e_ = mxq(f64(e), 0, "e4m3")
    y = dy_.T @ w_ + e_.T @ v_
    return f64(r) + y

@@ -1,0 +1,114 @@
+from contextlib import ExitStack
+
+import concourse.mybir as mybir
+
+K, L, D, T = 1024, 1024, 512, 512
+
+F32 = mybir.dt.float32
+BF16 = mybir.dt.bfloat16
+U32 = mybir.dt.uint32
+U8 = mybir.dt.uint8
+E4M3 = mybir.dt.float8_e4m3fn_x4
+E5M2 = mybir.dt.float8_e5m2_x4
+
+P = 128
+PACK = 4
+K_PASS = P * PACK
+T_TILE = 128
+
+FLOPS = 2 * (K + L) * D * T
+
+
+def tile_mix_aux_tm_res_kernel(tc, w, dy, v, e, r, out):
+    nc = tc.nc
+    with ExitStack() as ctx:
+        keep = ctx.enter_context(tc.tile_pool(name="keep", bufs=1))
+        psum = ctx.enter_context(tc.psum_pool(name="psum", bufs=1))
+        ctx.enter_context(tc.manual_schedule())
+
+        operands = {"w": (w, E4M3), "dy": (dy, E5M2), "v": (v, E4M3), "e": (e, E4M3)}
+        codes, planes = {}, {}
+        for name in operands:
+            for c in range(2):
+                codes[name, c] = keep.tile([P, 512], U32, name="codes_%s%d" % (name, c), align_bytes=64)
+                planes[name, c] = keep.tile([P, 512], U8, name="plane_%s%d" % (name, c), align_bytes=64)
+        raws = {}
+        residuals = {}
+        for i, (name, c, n, first, width, queue) in enumerate([["w",0,1,0,512,0],["w",1,1,0,512,0],["v",0,1,0,512,0],["v",1,1,0,512,0],["dy",0,1,0,512,0],["dy",1,1,0,512,0],["e",0,1,0,512,0],["e",1,1,0,512,0],["r",0,2,0,512,0],["r",2,2,0,512,0]]):
+            eng = nc.sync if queue == 0 else nc.scalar
+            if name == "r":
+                residual = keep.tile([P, n, D], F32, name="residual_%d" % i, align_bytes=64)
+                eng.dma_start(out=residual[:], in_=r[c * T_TILE : (c + n) * T_TILE, :].rearrange("(m p) x -> p m x", p=P))
+                for m in range(n):
+                    residuals[c + m] = residual[:, m, :]
+            else:
+                raw = keep.tile([P, n, PACK, width], F32, name="raw_%d" % i, align_bytes=64)
+                rows = operands[name][0][c * K_PASS : (c + n) * K_PASS, first : first + width]
+                if n == 1:
+                    eng.dma_start(out=raw[:, 0], in_=rows.rearrange("(p j) x -> p j x", j=PACK))
+                else:
+                    eng.dma_start(out=raw[:].rearrange("p c j x -> p c (j x)"), in_=rows.rearrange("(c p j) x -> p c (j x)", j=PACK, p=P))
+                for m in range(n):
+                    raws[name, c + m, first] = raw[:, m]
+
+        sums = [psum.tile([T_TILE, D], F32, name="sum_%d" % m) for m in range(T // T_TILE)]
+        seen = {}
+
+        def multiply(stationary, moving, kind, c, m):
+            t_cols = slice(m * T_TILE, (m + 1) * T_TILE)
+            n = seen.get(m, 0)
+            seen[m] = n + 1
+            nc.tensor.matmul_mx(
+                out=sums[m][:],
+                lhsT=codes[stationary, c][:, t_cols].bitcast(kind),
+                lhsT_scale=planes[stationary, c][:, t_cols],
+                rhs=codes[moving, c][:].bitcast(E4M3),
+                rhs_scale=planes[moving, c][:],
+                start=n == 0,
+                stop=n == 3,
+            )
+
+        grouped = {}
+        for step in [["c","w",0,0,512,320],["q","w",0,0,512],["c","w",1,0,512,320],["q","w",1,0,512],["c","v",0,0,512,320],["q","v",0,0,512],["c","v",1,0,512,320],["q","v",1,0,512],["c","dy",0,0,512,320],["q","dy",0,0,512],["dy",0,[0,1,2,3]],["c","dy",1,0,512,320],["q","dy",1,0,512],["dy",1,[0,1,2,3]],["c","e",0,0,512,320],["q","e",0,0,512],["e",0,[0,1,2,3]],["c","e",1,0,128,128],["c","e",1,256,128,0],["c","e",1,128,128,128],["c","e",1,384,128,0],["q","e",1,0,128],["e",1,[0]],["q","e",1,128,128],["e",1,[1]],["q","e",1,256,128],["e",1,[2]],["q","e",1,384,128],["e",1,[3]],["add",0,1],["add",1,1],["add",2,1],["add",3,2]]:
+            if step[0] == "c":
+                name, c, first, width, share = step[1:]
+                g = keep.tile([P, width, PACK], BF16, name="grouped_%s%d_%d" % (name, c, first), align_bytes=64)
+                grouped[name, c, first] = g
+                source = raws[name, c, 0][:, :, first : first + width].rearrange("p j (x i) -> p x j i", i=4)
+                target = g[:].rearrange("p (x i) j -> p x j i", i=4)
+                share //= 4
+                width //= 4
+                if share:
+                    nc.vector.tensor_copy(out=target[:, :share], in_=source[:, :share])
+                if share < width:
+                    nc.scalar.copy(out=target[:, share:], in_=source[:, share:])
+            elif step[0] == "q":
+                name, c, first, width = step[1:]
+                cols = slice(first, first + width)
+                nc.vector.quantize_mx(
+                    out=codes[name, c][:, cols].bitcast(operands[name][1]),
+                    scales=planes[name, c][:, cols],
+                    in_=grouped[name, c, first][:].rearrange("p x j -> p (x j)"),
+                )
+            elif step[0] == "dy":
+                for m in step[2]:
+                    multiply("dy", "w", E5M2, step[1], m)
+            elif step[0] == "e":
+                for m in step[2]:
+                    multiply("e", "v", E4M3, step[1], m)
+            elif step[0] == "gadd":
+                m = step[1]
+                plain = keep.tile([P, D], F32, name="plain_%d" % m, align_bytes=64)
+                nc.scalar.copy(out=plain[:], in_=sums[m][:])
+                result = keep.tile([P, D], F32, name="result_%d" % m, align_bytes=64)
+                nc.gpsimd.tensor_tensor(out=result[:], in0=plain[:], in1=residuals[m], op=mybir.AluOpType.add)
+                nc.scalar.dma_start(out=out[m * T_TILE : (m + 1) * T_TILE, :], in_=result[:])
+            elif step[0] == "add":
+                m, parts = step[1:]
+                width = D // parts
+                for h in range(parts):
+                    result = keep.tile([P, width], F32, name="result_%d_%d" % (m, h), align_bytes=64)
+                    cols = slice(h * width, (h + 1) * width)
+                    nc.vector.tensor_tensor(out=result[:], in0=sums[m][:, cols], in1=residuals[m][:, cols], op=mybir.AluOpType.add)
+                    eng = nc.scalar if h == 1 else nc.sync
+                    eng.dma_start(out=out[m * T_TILE : (m + 1) * T_TILE, cols], in_=result[:])

@@ -15,6 +15,7 @@ P = 128
 PACK = 4
 K_PASS = P * PACK
 T_TILE = 128
+RUN = 4
 
 FLOPS = 2 * (K + L) * D * T
 
@@ -27,88 +28,105 @@ def tile_mix_aux_tm_res_kernel(tc, w, dy, v, e, r, out):
         ctx.enter_context(tc.manual_schedule())
 
         operands = {"w": (w, E4M3), "dy": (dy, E5M2), "v": (v, E4M3), "e": (e, E4M3)}
+        partner = {"dy": "w", "e": "v"}
         codes, planes = {}, {}
         for name in operands:
             for c in range(2):
                 codes[name, c] = keep.tile([P, 512], U32, name="codes_%s%d" % (name, c), align_bytes=64)
                 planes[name, c] = keep.tile([P, 512], U8, name="plane_%s%d" % (name, c), align_bytes=64)
-        raws = {}
-        residuals = {}
-        for i, (name, c, n, first, width, queue) in enumerate([["w",0,1,0,512,0],["w",1,1,0,512,0],["v",0,1,0,512,0],["v",1,1,0,512,0],["dy",0,1,0,512,0],["dy",1,1,0,512,0],["e",0,1,0,512,0],["e",1,1,0,512,0],["r",0,2,0,512,0],["r",2,2,0,512,0]]):
-            eng = nc.sync if queue == 0 else nc.scalar
-            if name == "r":
-                residual = keep.tile([P, n, D], F32, name="residual_%d" % i, align_bytes=64)
-                eng.dma_start(out=residual[:], in_=r[c * T_TILE : (c + n) * T_TILE, :].rearrange("(m p) x -> p m x", p=P))
-                for m in range(n):
-                    residuals[c + m] = residual[:, m, :]
-            else:
-                raw = keep.tile([P, n, PACK, width], F32, name="raw_%d" % i, align_bytes=64)
-                rows = operands[name][0][c * K_PASS : (c + n) * K_PASS, first : first + width]
-                if n == 1:
-                    eng.dma_start(out=raw[:, 0], in_=rows.rearrange("(p j) x -> p j x", j=PACK))
-                else:
-                    eng.dma_start(out=raw[:].rearrange("p c j x -> p c (j x)"), in_=rows.rearrange("(c p j) x -> p c (j x)", j=PACK, p=P))
-                for m in range(n):
-                    raws[name, c + m, first] = raw[:, m]
-
         sums = [psum.tile([T_TILE, D], F32, name="sum_%d" % m) for m in range(T // T_TILE)]
-        seen = {}
+        raws, grouped, residuals, seen = {}, {}, {}, {}
 
-        def multiply(stationary, moving, kind, c, m):
-            t_cols = slice(m * T_TILE, (m + 1) * T_TILE)
-            n = seen.get(m, 0)
-            seen[m] = n + 1
-            nc.tensor.matmul_mx(
-                out=sums[m][:],
-                lhsT=codes[stationary, c][:, t_cols].bitcast(kind),
-                lhsT_scale=planes[stationary, c][:, t_cols],
-                rhs=codes[moving, c][:].bitcast(E4M3),
-                rhs_scale=planes[moving, c][:],
-                start=n == 0,
-                stop=n == 3,
+        def load(name, c, first, width):
+            raw = keep.tile([P, PACK, width], F32, name="raw_%s%d_%d" % (name, c, first), align_bytes=64)
+            rows = operands[name][0][c * K_PASS : (c + 1) * K_PASS, first : first + width]
+            nc.sync.dma_start(out=raw[:], in_=rows.rearrange("(p j) x -> p j x", j=PACK))
+            raws[name, c, first] = raw[:]
+
+        def load_both(name):
+            raw = keep.tile([P, 2, PACK * 512], F32, name="raw_%s" % name, align_bytes=64)
+            nc.sync.dma_start(out=raw[:], in_=operands[name][0].rearrange("(c p j) x -> p c (j x)", j=PACK, p=P))
+            for c in range(2):
+                raws[name, c, 0] = raw[:, c, :].rearrange("p (j x) -> p j x", j=PACK)
+
+        def load_residual(m, tiles, first=0, width=D):
+            residual = keep.tile([P, tiles, width], F32, name="residual_%d_%d" % (m, first), align_bytes=64)
+            rows = r[m * T_TILE : (m + tiles) * T_TILE, first : first + width]
+            nc.sync.dma_start(out=residual[:], in_=rows.rearrange("(m p) x -> p m x", p=P))
+            for i in range(tiles):
+                residuals[m + i, first] = residual[:, i, :]
+
+        def interleave(name, c, first, width, on_vector, loaded_at=None):
+            g = keep.tile([P, width, PACK], BF16, name="grouped_%s%d_%d" % (name, c, first), align_bytes=64)
+            grouped[name, c, first] = g
+            base = first if loaded_at is None else loaded_at
+            source = raws[name, c, base][:, :, first - base : first - base + width].rearrange("p j (x i) -> p x j i", i=RUN)
+            target = g[:].rearrange("p (x i) j -> p x j i", i=RUN)
+            cut = on_vector // RUN
+            if cut > 0:
+                nc.vector.tensor_copy(out=target[:, :cut], in_=source[:, :cut])
+            if cut < width // RUN:
+                nc.scalar.copy(out=target[:, cut:], in_=source[:, cut:])
+
+        def quantise(name, c, first, width):
+            cols = slice(first, first + width)
+            nc.vector.quantize_mx(
+                out=codes[name, c][:, cols].bitcast(operands[name][1]),
+                scales=planes[name, c][:, cols],
+                in_=grouped[name, c, first][:].rearrange("p x j -> p (x j)"),
             )
 
-        grouped = {}
-        for step in [["c","w",0,0,512,320],["q","w",0,0,512],["c","w",1,0,512,320],["q","w",1,0,512],["c","v",0,0,512,320],["q","v",0,0,512],["c","v",1,0,512,320],["q","v",1,0,512],["c","dy",0,0,512,320],["q","dy",0,0,512],["dy",0,[0,1,2,3]],["c","dy",1,0,512,320],["q","dy",1,0,512],["dy",1,[0,1,2,3]],["c","e",0,0,512,320],["q","e",0,0,512],["e",0,[0,1,2,3]],["c","e",1,0,128,128],["c","e",1,256,128,0],["c","e",1,128,128,128],["c","e",1,384,128,0],["q","e",1,0,128],["e",1,[0]],["q","e",1,128,128],["e",1,[1]],["q","e",1,256,128],["e",1,[2]],["q","e",1,384,128],["e",1,[3]],["add",0,1],["add",1,1],["add",2,1],["add",3,2]]:
-            if step[0] == "c":
-                name, c, first, width, share = step[1:]
-                g = keep.tile([P, width, PACK], BF16, name="grouped_%s%d_%d" % (name, c, first), align_bytes=64)
-                grouped[name, c, first] = g
-                source = raws[name, c, 0][:, :, first : first + width].rearrange("p j (x i) -> p x j i", i=4)
-                target = g[:].rearrange("p (x i) j -> p x j i", i=4)
-                share //= 4
-                width //= 4
-                if share:
-                    nc.vector.tensor_copy(out=target[:, :share], in_=source[:, :share])
-                if share < width:
-                    nc.scalar.copy(out=target[:, share:], in_=source[:, share:])
-            elif step[0] == "q":
-                name, c, first, width = step[1:]
-                cols = slice(first, first + width)
-                nc.vector.quantize_mx(
-                    out=codes[name, c][:, cols].bitcast(operands[name][1]),
-                    scales=planes[name, c][:, cols],
-                    in_=grouped[name, c, first][:].rearrange("p x j -> p (x j)"),
+        def multiply(name, c, tiles):
+            for m in tiles:
+                t_cols = slice(m * T_TILE, (m + 1) * T_TILE)
+                n = seen.get(m, 0)
+                seen[m] = n + 1
+                nc.tensor.matmul_mx(
+                    out=sums[m][:],
+                    lhsT=codes[name, c][:, t_cols].bitcast(operands[name][1]),
+                    lhsT_scale=planes[name, c][:, t_cols],
+                    rhs=codes[partner[name], c][:].bitcast(E4M3),
+                    rhs_scale=planes[partner[name], c][:],
+                    start=n == 0,
+                    stop=n == 3,
                 )
-            elif step[0] == "dy":
-                for m in step[2]:
-                    multiply("dy", "w", E5M2, step[1], m)
-            elif step[0] == "e":
-                for m in step[2]:
-                    multiply("e", "v", E4M3, step[1], m)
-            elif step[0] == "gadd":
-                m = step[1]
-                plain = keep.tile([P, D], F32, name="plain_%d" % m, align_bytes=64)
-                nc.scalar.copy(out=plain[:], in_=sums[m][:])
-                result = keep.tile([P, D], F32, name="result_%d" % m, align_bytes=64)
-                nc.gpsimd.tensor_tensor(out=result[:], in0=plain[:], in1=residuals[m], op=mybir.AluOpType.add)
-                nc.scalar.dma_start(out=out[m * T_TILE : (m + 1) * T_TILE, :], in_=result[:])
-            elif step[0] == "add":
-                m, parts = step[1:]
-                width = D // parts
-                for h in range(parts):
-                    result = keep.tile([P, width], F32, name="result_%d_%d" % (m, h), align_bytes=64)
-                    cols = slice(h * width, (h + 1) * width)
-                    nc.vector.tensor_tensor(out=result[:], in0=sums[m][:, cols], in1=residuals[m][:, cols], op=mybir.AluOpType.add)
-                    eng = nc.scalar if h == 1 else nc.sync
-                    eng.dma_start(out=out[m * T_TILE : (m + 1) * T_TILE, cols], in_=result[:])
+
+        def finish(m, first, width, queue, loaded_at=0):
+            result = keep.tile([P, width], F32, name="result_%d_%d" % (m, first), align_bytes=64)
+            cols = slice(first, first + width)
+            residual = residuals[m, loaded_at][:, first - loaded_at : first - loaded_at + width]
+            nc.vector.tensor_tensor(out=result[:], in0=sums[m][:, cols], in1=residual, op=mybir.AluOpType.add)
+            queue.dma_start(out=out[m * T_TILE : (m + 1) * T_TILE, cols], in_=result[:])
+
+        load_both("w")
+        load_both("v")
+        for c in range(2):
+            load("dy", c, 0, 512)
+        load("e", 0, 0, 512)
+        load("e", 1, 0, 512)
+        load_residual(0, 2)
+        load_residual(2, 2)
+        for name in ("w", "v"):
+            for c in range(2):
+                interleave(name, c, 0, 512, 256)
+            for c in range(2):
+                quantise(name, c, 0, 512)
+        for c in range(2):
+            interleave("dy", c, 0, 512, 320)
+            quantise("dy", c, 0, 512)
+            multiply("dy", c, range(4))
+        interleave("e", 0, 0, 512, 320)
+        quantise("e", 0, 0, 512)
+        multiply("e", 0, range(4))
+        interleave("e", 1, 0, 128, 128)
+        interleave("e", 1, 256, 128, 0, loaded_at=0)
+        interleave("e", 1, 128, 128, 128, loaded_at=0)
+        interleave("e", 1, 384, 128, 0, loaded_at=0)
+        for m in range(4):
+            quantise("e", 1, 128*m, 128)
+            multiply("e", 1, (m,))
+        finish(0, 0, 512, nc.sync)
+        finish(1, 0, 512, nc.sync)
+        finish(2, 0, 512, nc.sync)
+        finish(3, 0, 256, nc.sync)
+        finish(3, 256, 256, nc.scalar)

@@ -103,30 +103,45 @@ def tile_mix_aux_tm_res_kernel(tc, w, dy, v, e, r, out):
         for c in range(2):
             load("dy", c, 0, 512)
         load("e", 0, 0, 512)
-        load("e", 1, 0, 512)
-        load_residual(0, 2)
-        load_residual(2, 2)
+        load("e", 1, 0, 256)
+        load("e", 1, 256, 256)
+        load_residual(0, 1)
+        load_residual(1, 1)
+        load_residual(2, 1)
+        load_residual(3, 1)
+
         for name in ("w", "v"):
             for c in range(2):
                 interleave(name, c, 0, 512, 256)
-            for c in range(2):
-                quantise(name, c, 0, 512)
-        for c in range(2):
-            interleave("dy", c, 0, 512, 320)
-            quantise("dy", c, 0, 512)
-            multiply("dy", c, range(4))
-        interleave("e", 0, 0, 512, 320)
-        quantise("e", 0, 0, 512)
-        multiply("e", 0, range(4))
-        interleave("e", 1, 0, 128, 128)
-        interleave("e", 1, 256, 128, 0, loaded_at=0)
-        interleave("e", 1, 128, 128, 128, loaded_at=0)
-        interleave("e", 1, 384, 128, 0, loaded_at=0)
-        for m in range(4):
-            quantise("e", 1, 128*m, 128)
-            multiply("e", 1, (m,))
+            quantise(name, 0, 0, 512)
+            if name == "w":
+                quantise(name, 1, 0, 512)
+        interleave("dy", 0, 0, 512, 320)
+        quantise("dy", 0, 0, 512)
+        multiply("dy", 0, range(4))
+        quantise("v", 1, 0, 512)
+
+        interleave("dy", 1, 0, 512, 320)
+        quantise("dy", 1, 0, 512)
+        multiply("dy", 1, range(4))
+        interleave("e", 0, 0, 256, 160)
+        interleave("e", 0, 256, 256, 128, loaded_at=0)
+        quantise("e", 0, 0, 256)
+        multiply("e", 0, (0, 1))
+        interleave("e", 1, 0, 256, 160)
+        quantise("e", 0, 256, 256)
+        multiply("e", 0, (2,))
+        quantise("e", 1, 0, 256)
+        multiply("e", 1, (0, 1))
+        multiply("e", 0, (3,))
+
+        interleave("e", 1, 256, 128, 80)
+        interleave("e", 1, 384, 128, 80, loaded_at=256)
+        quantise("e", 1, 256, 128)
+        multiply("e", 1, (2,))
+        quantise("e", 1, 384, 128)
+        multiply("e", 1, (3,))
         finish(0, 0, 512, nc.sync)
         finish(1, 0, 512, nc.sync)
         finish(2, 0, 512, nc.sync)
-        finish(3, 0, 256, nc.sync)
-        finish(3, 256, 256, nc.scalar)
+        finish(3, 0, 512, nc.sync)

@@ -37,10 +37,10 @@ def tile_mix_aux_tm_res_kernel(tc, w, dy, v, e, r, out):
         sums = [psum.tile([T_TILE, D], F32, name="sum_%d" % m) for m in range(T // T_TILE)]
         raws, grouped, residuals, seen = {}, {}, {}, {}
 
-        def load(name, c, first, width):
+        def load(name, c, first, width, queue=nc.sync):
             raw = keep.tile([P, PACK, width], F32, name="raw_%s%d_%d" % (name, c, first), align_bytes=64)
             rows = operands[name][0][c * K_PASS : (c + 1) * K_PASS, first : first + width]
-            nc.sync.dma_start(out=raw[:], in_=rows.rearrange("(p j) x -> p j x", j=PACK))
+            queue.dma_start(out=raw[:], in_=rows.rearrange("(p j) x -> p j x", j=PACK))
             raws[name, c, first] = raw[:]
 
         def load_both(name):
@@ -48,6 +48,14 @@ def tile_mix_aux_tm_res_kernel(tc, w, dy, v, e, r, out):
             nc.sync.dma_start(out=raw[:], in_=operands[name][0].rearrange("(c p j) x -> p c (j x)", j=PACK, p=P))
             for c in range(2):
                 raws[name, c, 0] = raw[:, c, :].rearrange("p (j x) -> p j x", j=PACK)
+
+        def load_staggered(name, c, first):
+            raw = keep.tile([P, 2, 2 * 512], F32, name="raw_%s%d" % (name, c), align_bytes=64)
+            rows = operands[name][0][c * K_PASS : (c + 1) * K_PASS, :].rearrange("(p h j) x -> p h (j x)", h=2, j=2)
+            cut = 512 + first
+            nc.sync.dma_start(out=raw[:, :, :cut], in_=rows[:, :, :cut])
+            nc.sync.dma_start(out=raw[:, :, cut:], in_=rows[:, :, cut:])
+            raws[name, c, 0] = raw[:].rearrange("p h (j x) -> p (h j) x", j=2)
 
         def load_residual(m, tiles, first=0, width=D):
             residual = keep.tile([P, tiles, width], F32, name="residual_%d_%d" % (m, first), align_bytes=64)
@@ -90,6 +98,15 @@ def tile_mix_aux_tm_res_kernel(tc, w, dy, v, e, r, out):
                     start=n == 0,
                     stop=n == 3,
                 )
+
+        def finish_shared(m, cut):
+            result = keep.tile([P, D], F32, name="result_%d" % m, align_bytes=64)
+            plain = keep.tile([P, D - cut], F32, name="plain_%d" % m, align_bytes=64)
+            residual = residuals[m, 0]
+            nc.scalar.copy(out=plain[:], in_=sums[m][:, cut:])
+            nc.gpsimd.tensor_tensor(out=result[:, cut:], in0=plain[:], in1=residual[:, cut:], op=mybir.AluOpType.add)
+            nc.vector.tensor_tensor(out=result[:, :cut], in0=sums[m][:, :cut], in1=residual[:, :cut], op=mybir.AluOpType.add)
+            nc.sync.dma_start(out=out[m * T_TILE : (m + 1) * T_TILE, :], in_=result[:])
 
         def finish(m, first, width, queue, loaded_at=0):
             result = keep.tile([P, width], F32, name="result_%d_%d" % (m, first), align_bytes=64)
@@ -141,7 +158,6 @@ def tile_mix_aux_tm_res_kernel(tc, w, dy, v, e, r, out):
         multiply("e", 1, (2,))
         quantise("e", 1, 384, 128)
         multiply("e", 1, (3,))
-        finish(0, 0, 512, nc.sync)
-        finish(1, 0, 512, nc.sync)
-        finish(2, 0, 512, nc.sync)
-        finish(3, 0, 512, nc.sync)
+
+        for m in range(4):
+            finish_shared(m, 384)

@@ -153,11 +153,12 @@ def tile_mix_aux_tm_res_kernel(tc, w, dy, v, e, r, out):
         multiply("e", 0, (3,))
 
         interleave("e", 1, 256, 128, 80)
-        interleave("e", 1, 384, 128, 80, loaded_at=256)
+        interleave("e", 1, 384, 128, 48, loaded_at=256)
         quantise("e", 1, 256, 128)
         multiply("e", 1, (2,))
+        finish(0, 0, 512, nc.sync)
         quantise("e", 1, 384, 128)
         multiply("e", 1, (3,))
-
-        for m in range(4):
+        for m in (1, 2):
             finish_shared(m, 384)
+        finish(3, 0, 512, nc.sync)

@@ -32,40 +32,32 @@ def tile_mix_aux_tm_res_kernel(tc, w, dy, v, e, r, out):
         codes, planes = {}, {}
         for name in operands:
             for c in range(2):
-                codes[name, c] = keep.tile([P, 512], U32, name="codes_%s%d" % (name, c), align_bytes=64)
-                planes[name, c] = keep.tile([P, 512], U8, name="plane_%s%d" % (name, c), align_bytes=64)
+                codes[name, c] = keep.tile([P, 512], U32, name="codes_%s%d" % (name, c), align_bytes=256)
+                planes[name, c] = keep.tile([P, 512], U8, name="plane_%s%d" % (name, c), align_bytes=256)
         sums = [psum.tile([T_TILE, D], F32, name="sum_%d" % m) for m in range(T // T_TILE)]
         raws, grouped, residuals, seen = {}, {}, {}, {}
 
         def load(name, c, first, width, queue=nc.sync):
-            raw = keep.tile([P, PACK, width], F32, name="raw_%s%d_%d" % (name, c, first), align_bytes=64)
+            raw = keep.tile([P, PACK, width], F32, name="raw_%s%d_%d" % (name, c, first), align_bytes=256)
             rows = operands[name][0][c * K_PASS : (c + 1) * K_PASS, first : first + width]
             queue.dma_start(out=raw[:], in_=rows.rearrange("(p j) x -> p j x", j=PACK))
             raws[name, c, first] = raw[:]
 
         def load_both(name):
-            raw = keep.tile([P, 2, PACK * 512], F32, name="raw_%s" % name, align_bytes=64)
+            raw = keep.tile([P, 2, PACK * 512], F32, name="raw_%s" % name, align_bytes=256)
             nc.sync.dma_start(out=raw[:], in_=operands[name][0].rearrange("(c p j) x -> p c (j x)", j=PACK, p=P))
             for c in range(2):
                 raws[name, c, 0] = raw[:, c, :].rearrange("p (j x) -> p j x", j=PACK)
 
-        def load_staggered(name, c, first):
-            raw = keep.tile([P, 2, 2 * 512], F32, name="raw_%s%d" % (name, c), align_bytes=64)
-            rows = operands[name][0][c * K_PASS : (c + 1) * K_PASS, :].rearrange("(p h j) x -> p h (j x)", h=2, j=2)
-            cut = 512 + first
-            nc.sync.dma_start(out=raw[:, :, :cut], in_=rows[:, :, :cut])
-            nc.sync.dma_start(out=raw[:, :, cut:], in_=rows[:, :, cut:])
-            raws[name, c, 0] = raw[:].rearrange("p h (j x) -> p (h j) x", j=2)
-
         def load_residual(m, tiles, first=0, width=D):
-            residual = keep.tile([P, tiles, width], F32, name="residual_%d_%d" % (m, first), align_bytes=64)
+            residual = keep.tile([P, tiles, width], F32, name="residual_%d_%d" % (m, first), align_bytes=256)
             rows = r[m * T_TILE : (m + tiles) * T_TILE, first : first + width]
             nc.sync.dma_start(out=residual[:], in_=rows.rearrange("(m p) x -> p m x", p=P))
             for i in range(tiles):
                 residuals[m + i, first] = residual[:, i, :]
 
         def interleave(name, c, first, width, on_vector, loaded_at=None):
-            g = keep.tile([P, width, PACK], BF16, name="grouped_%s%d_%d" % (name, c, first), align_bytes=64)
+            g = keep.tile([P, width, PACK], BF16, name="grouped_%s%d_%d" % (name, c, first), align_bytes=256)
             grouped[name, c, first] = g
             base = first if loaded_at is None else loaded_at
             source = raws[name, c, base][:, :, first - base : first - base + width].rearrange("p j (x i) -> p x j i", i=RUN)
@@ -100,8 +92,8 @@ def tile_mix_aux_tm_res_kernel(tc, w, dy, v, e, r, out):
                 )
 
         def finish_shared(m, cut):
-            result = keep.tile([P, D], F32, name="result_%d" % m, align_bytes=64)
-            plain = keep.tile([P, D - cut], F32, name="plain_%d" % m, align_bytes=64)
+            result = keep.tile([P, D], F32, name="result_%d" % m, align_bytes=256)
+            plain = keep.tile([P, D - cut], F32, name="plain_%d" % m, align_bytes=256)
             residual = residuals[m, 0]
             nc.scalar.copy(out=plain[:], in_=sums[m][:, cut:])
             nc.gpsimd.tensor_tensor(out=result[:, cut:], in0=plain[:], in1=residual[:, cut:], op=mybir.AluOpType.add)
@@ -109,7 +101,7 @@ def tile_mix_aux_tm_res_kernel(tc, w, dy, v, e, r, out):
             nc.sync.dma_start(out=out[m * T_TILE : (m + 1) * T_TILE, :], in_=result[:])
 
         def finish(m, first, width, queue, loaded_at=0):
-            result = keep.tile([P, width], F32, name="result_%d_%d" % (m, first), align_bytes=64)
+            result = keep.tile([P, width], F32, name="result_%d_%d" % (m, first), align_bytes=256)
             cols = slice(first, first + width)
             residual = residuals[m, loaded_at][:, first - loaded_at : first - loaded_at + width]
             nc.vector.tensor_tensor(out=result[:], in0=sums[m][:, cols], in1=residual, op=mybir.AluOpType.add)

@@ -16,6 +16,7 @@ PACK = 4
 K_PASS = P * PACK
 T_TILE = 128
 RUN = 4
+CUT = 384
 
 FLOPS = 2 * (K + L) * D * T
 
@@ -35,7 +36,7 @@ def tile_mix_aux_tm_res_kernel(tc, w, dy, v, e, r, out):
                 codes[name, c] = keep.tile([P, 512], U32, name="codes_%s%d" % (name, c), align_bytes=256)
                 planes[name, c] = keep.tile([P, 512], U8, name="plane_%s%d" % (name, c), align_bytes=256)
         sums = [psum.tile([T_TILE, D], F32, name="sum_%d" % m) for m in range(T // T_TILE)]
-        raws, grouped, residuals, seen = {}, {}, {}, {}
+        raws, grouped, residuals, plains, seen = {}, {}, {}, {}, {}
 
         def load(name, c, first, width, queue=nc.sync):
             raw = keep.tile([P, PACK, width], F32, name="raw_%s%d_%d" % (name, c, first), align_bytes=256)
@@ -56,24 +57,27 @@ def tile_mix_aux_tm_res_kernel(tc, w, dy, v, e, r, out):
             for i in range(tiles):
                 residuals[m + i, first] = residual[:, i, :]
 
-        def interleave(name, c, first, width, on_vector, loaded_at=None):
-            g = keep.tile([P, width, PACK], BF16, name="grouped_%s%d_%d" % (name, c, first), align_bytes=256)
-            grouped[name, c, first] = g
-            base = first if loaded_at is None else loaded_at
+        def interleave(engine, name, c, first, width):
+            if (name, c) not in grouped:
+                grouped[name, c] = keep.tile([P, 512, PACK], BF16, name="grouped_%s%d" % (name, c), align_bytes=256)
+            base = max(start for key, part, start in raws if (key, part) == (name, c) and start <= first)
             source = raws[name, c, base][:, :, first - base : first - base + width].rearrange("p j (x i) -> p x j i", i=RUN)
-            target = g[:].rearrange("p (x i) j -> p x j i", i=RUN)
-            cut = on_vector // RUN
-            if cut > 0:
-                nc.vector.tensor_copy(out=target[:, :cut], in_=source[:, :cut])
-            if cut < width // RUN:
-                nc.scalar.copy(out=target[:, cut:], in_=source[:, cut:])
+            target = grouped[name, c][:, first : first + width, :].rearrange("p (x i) j -> p x j i", i=RUN)
+            if engine == "vector":
+                nc.vector.tensor_copy(out=target, in_=source)
+            else:
+                nc.scalar.copy(out=target, in_=source)
+
+        def shared(name, c, first, width, on_vector):
+            interleave("vector", name, c, first, on_vector)
+            interleave("scalar", name, c, first + on_vector, width - on_vector)
 
         def quantise(name, c, first, width):
             cols = slice(first, first + width)
             nc.vector.quantize_mx(
                 out=codes[name, c][:, cols].bitcast(operands[name][1]),
                 scales=planes[name, c][:, cols],
-                in_=grouped[name, c, first][:].rearrange("p x j -> p (x j)"),
+                in_=grouped[name, c][:, cols, :].rearrange("p x j -> p (x j)"),
             )
 
         def multiply(name, c, tiles):
@@ -91,12 +95,15 @@ def tile_mix_aux_tm_res_kernel(tc, w, dy, v, e, r, out):
                     stop=n == 3,
                 )
 
+        def copy_out(m, cut):
+            plain = keep.tile([P, D - cut], F32, name="plain_%d" % m, align_bytes=256)
+            nc.scalar.copy(out=plain[:], in_=sums[m][:, cut:])
+            plains[m] = plain
+
         def finish_shared(m, cut):
             result = keep.tile([P, D], F32, name="result_%d" % m, align_bytes=256)
-            plain = keep.tile([P, D - cut], F32, name="plain_%d" % m, align_bytes=256)
             residual = residuals[m, 0]
-            nc.scalar.copy(out=plain[:], in_=sums[m][:, cut:])
-            nc.gpsimd.tensor_tensor(out=result[:, cut:], in0=plain[:], in1=residual[:, cut:], op=mybir.AluOpType.add)
+            nc.gpsimd.tensor_tensor(out=result[:, cut:], in0=plains[m][:], in1=residual[:, cut:], op=mybir.AluOpType.add)
             nc.vector.tensor_tensor(out=result[:, :cut], in0=sums[m][:, :cut], in1=residual[:, :cut], op=mybir.AluOpType.add)
             nc.sync.dma_start(out=out[m * T_TILE : (m + 1) * T_TILE, :], in_=result[:])
 
@@ -114,43 +121,42 @@ def tile_mix_aux_tm_res_kernel(tc, w, dy, v, e, r, out):
         load("e", 0, 0, 512)
         load("e", 1, 0, 256)
         load("e", 1, 256, 256)
-        load_residual(0, 1)
-        load_residual(1, 1)
-        load_residual(2, 1)
-        load_residual(3, 1)
+        for m in range(4):
+            load_residual(m, 1)
 
-        for name in ("w", "v"):
-            for c in range(2):
-                interleave(name, c, 0, 512, 256)
-            quantise(name, 0, 0, 512)
-            if name == "w":
-                quantise(name, 1, 0, 512)
-        interleave("dy", 0, 0, 512, 320)
+        for c in range(2):
+            shared("w", c, 0, 512, 320)
+        for c in range(2):
+            quantise("w", c, 0, 512)
+        for c in range(2):
+            shared("v", c, 0, 512, 320)
+        quantise("v", 0, 0, 512)
+        shared("dy", 0, 0, 512, 320)
+        quantise("v", 1, 0, 512)
         quantise("dy", 0, 0, 512)
         multiply("dy", 0, range(4))
-        quantise("v", 1, 0, 512)
-
-        interleave("dy", 1, 0, 512, 320)
+        shared("dy", 1, 0, 512, 320)
         quantise("dy", 1, 0, 512)
         multiply("dy", 1, range(4))
-        interleave("e", 0, 0, 256, 160)
-        interleave("e", 0, 256, 256, 128, loaded_at=0)
+        shared("e", 0, 0, 256, 160)
+        shared("e", 0, 256, 256, 128)
         quantise("e", 0, 0, 256)
         multiply("e", 0, (0, 1))
-        interleave("e", 1, 0, 256, 160)
+        shared("e", 1, 0, 256, 160)
         quantise("e", 0, 256, 256)
         multiply("e", 0, (2,))
         quantise("e", 1, 0, 256)
         multiply("e", 1, (0, 1))
         multiply("e", 0, (3,))
 
-        interleave("e", 1, 256, 128, 80)
-        interleave("e", 1, 384, 128, 48, loaded_at=256)
+        shared("e", 1, 256, 128, 80)
+        shared("e", 1, 384, 128, 48)
         quantise("e", 1, 256, 128)
         multiply("e", 1, (2,))
         finish(0, 0, 512, nc.sync)
         quantise("e", 1, 384, 128)
         multiply("e", 1, (3,))
         for m in (1, 2):
-            finish_shared(m, 384)
+            copy_out(m, CUT)
+            finish_shared(m, CUT)
         finish(3, 0, 512, nc.sync)

@@ -120,7 +120,8 @@ def tile_mix_aux_tm_res_kernel(tc, w, dy, v, e, r, out):
             load("dy", c, 0, 512)
         load("e", 0, 0, 512)
         load("e", 1, 0, 256)
-        load("e", 1, 256, 256)
+        load("e", 1, 256, 128)
+        load("e", 1, 384, 128)
         for m in range(4):
             load_residual(m, 1)
 
@@ -139,7 +140,7 @@ def tile_mix_aux_tm_res_kernel(tc, w, dy, v, e, r, out):
         quantise("dy", 1, 0, 512)
         multiply("dy", 1, range(4))
         shared("e", 0, 0, 256, 160)
-        shared("e", 0, 256, 256, 128)
+        shared("e", 0, 256, 256, 96)
         quantise("e", 0, 0, 256)
         multiply("e", 0, (0, 1))
         shared("e", 1, 0, 256, 160)
@@ -148,14 +149,13 @@ def tile_mix_aux_tm_res_kernel(tc, w, dy, v, e, r, out):
         quantise("e", 1, 0, 256)
         multiply("e", 1, (0, 1))
         multiply("e", 0, (3,))
-
-        shared("e", 1, 256, 128, 80)
-        shared("e", 1, 384, 128, 48)
+        interleave("scalar", "e", 1, 256, 128)
+        shared("e", 1, 384, 128, 80)
         quantise("e", 1, 256, 128)
         multiply("e", 1, (2,))
-        finish(0, 0, 512, nc.sync)
         quantise("e", 1, 384, 128)
         multiply("e", 1, (3,))
+        finish(0, 0, 512, nc.sync)
         for m in (1, 2):
             copy_out(m, CUT)
             finish_shared(m, CUT)

@@ -30,13 +30,13 @@ def tile_mix_aux_tm_res_kernel(tc, w, dy, v, e, r, out):
 
         operands = {"w": (w, E4M3), "dy": (dy, E5M2), "v": (v, E4M3), "e": (e, E4M3)}
         partner = {"dy": "w", "e": "v"}
-        codes, planes = {}, {}
+        codes, planes, grouped = {}, {}, {}
         for name in operands:
-            for c in range(2):
-                codes[name, c] = keep.tile([P, 512], U32, name="codes_%s%d" % (name, c), align_bytes=256)
-                planes[name, c] = keep.tile([P, 512], U8, name="plane_%s%d" % (name, c), align_bytes=256)
+            codes[name] = keep.tile([P, 2, 512], U32, name="codes_%s" % name, align_bytes=256)
+            planes[name] = keep.tile([P, 2, 512], U8, name="plane_%s" % name, align_bytes=256)
+            grouped[name] = keep.tile([P, 2, 512, PACK], BF16, name="grouped_%s" % name, align_bytes=256)
         sums = [psum.tile([T_TILE, D], F32, name="sum_%d" % m) for m in range(T // T_TILE)]
-        raws, grouped, residuals, plains, seen = {}, {}, {}, {}, {}
+        raws, wholes, residuals, plains, seen = {}, {}, {}, {}, {}
 
         def load(name, c, first, width, queue=nc.sync):
             raw = keep.tile([P, PACK, width], F32, name="raw_%s%d_%d" % (name, c, first), align_bytes=256)
@@ -47,8 +47,21 @@ def tile_mix_aux_tm_res_kernel(tc, w, dy, v, e, r, out):
         def load_both(name):
             raw = keep.tile([P, 2, PACK * 512], F32, name="raw_%s" % name, align_bytes=256)
             nc.sync.dma_start(out=raw[:], in_=operands[name][0].rearrange("(c p j) x -> p c (j x)", j=PACK, p=P))
-            for c in range(2):
-                raws[name, c, 0] = raw[:, c, :].rearrange("p (j x) -> p j x", j=PACK)
+            wholes[name] = raw
+
+        def shared_both(name, on_vector):
+            source = wholes[name][:].rearrange("p c (j x i) -> p c x j i", j=PACK, i=RUN)
+            target = grouped[name][:].rearrange("p c (x i) j -> p c x j i", i=RUN)
+            cut = on_vector // RUN
+            nc.vector.tensor_copy(out=target[:, :, :cut], in_=source[:, :, :cut])
+            nc.scalar.copy(out=target[:, :, cut:], in_=source[:, :, cut:])
+
+        def quantise_both(name):
+            nc.vector.quantize_mx(
+                out=codes[name][:].rearrange("p c x -> p (c x)").bitcast(operands[name][1]),
+                scales=planes[name][:].rearrange("p c x -> p (c x)"),
+                in_=grouped[name][:].rearrange("p c x j -> p (c x j)"),
+            )
 
         def load_residual(m, tiles, first=0, width=D):
             residual = keep.tile([P, tiles, width], F32, name="residual_%d_%d" % (m, first), align_bytes=256)
@@ -58,11 +71,9 @@ def tile_mix_aux_tm_res_kernel(tc, w, dy, v, e, r, out):
                 residuals[m + i, first] = residual[:, i, :]
 
         def interleave(engine, name, c, first, width):
-            if (name, c) not in grouped:
-                grouped[name, c] = keep.tile([P, 512, PACK], BF16, name="grouped_%s%d" % (name, c), align_bytes=256)
             base = max(start for key, part, start in raws if (key, part) == (name, c) and start <= first)
             source = raws[name, c, base][:, :, first - base : first - base + width].rearrange("p j (x i) -> p x j i", i=RUN)
-            target = grouped[name, c][:, first : first + width, :].rearrange("p (x i) j -> p x j i", i=RUN)
+            target = grouped[name][:, c, first : first + width, :].rearrange("p (x i) j -> p x j i", i=RUN)
             if engine == "vector":
                 nc.vector.tensor_copy(out=target, in_=source)
             else:
@@ -75,9 +86,9 @@ def tile_mix_aux_tm_res_kernel(tc, w, dy, v, e, r, out):
         def quantise(name, c, first, width):
             cols = slice(first, first + width)
             nc.vector.quantize_mx(
-                out=codes[name, c][:, cols].bitcast(operands[name][1]),
-                scales=planes[name, c][:, cols],
-                in_=grouped[name, c][:, cols, :].rearrange("p x j -> p (x j)"),
+                out=codes[name][:, c, cols].bitcast(operands[name][1]),
+                scales=planes[name][:, c, cols],
+                in_=grouped[name][:, c, cols, :].rearrange("p x j -> p (x j)"),
             )
 
         def multiply(name, c, tiles):
@@ -87,10 +98,10 @@ def tile_mix_aux_tm_res_kernel(tc, w, dy, v, e, r, out):
                 seen[m] = n + 1
                 nc.tensor.matmul_mx(
                     out=sums[m][:],
-                    lhsT=codes[name, c][:, t_cols].bitcast(operands[name][1]),
-                    lhsT_scale=planes[name, c][:, t_cols],
-                    rhs=codes[partner[name], c][:].bitcast(E4M3),
-                    rhs_scale=planes[partner[name], c][:],
+                    lhsT=codes[name][:, c, t_cols].bitcast(operands[name][1]),
+                    lhsT_scale=planes[name][:, c, t_cols],
+                    rhs=codes[partner[name]][:, c, :].bitcast(E4M3),
+                    rhs_scale=planes[partner[name]][:, c, :],
                     start=n == 0,
                     stop=n == 3,
                 )
@@ -125,38 +136,40 @@ def tile_mix_aux_tm_res_kernel(tc, w, dy, v, e, r, out):
         for m in range(4):
             load_residual(m, 1)
 
-        for c in range(2):
-            shared("w", c, 0, 512, 320)
-        for c in range(2):
-            quantise("w", c, 0, 512)
-        for c in range(2):
-            shared("v", c, 0, 512, 320)
+        shared_both("w", 320)
+        quantise_both("w")
+        shared_both("v", 320)
         quantise("v", 0, 0, 512)
-        shared("dy", 0, 0, 512, 320)
+        for half in range(2):
+            shared("dy", 0, 256 * half, 256, 160)
+        for half in range(2):
+            quantise("dy", 0, 256 * half, 256)
+            multiply("dy", 0, (2 * half, 2 * half + 1))
         quantise("v", 1, 0, 512)
-        quantise("dy", 0, 0, 512)
-        multiply("dy", 0, range(4))
         shared("dy", 1, 0, 512, 320)
         quantise("dy", 1, 0, 512)
         multiply("dy", 1, range(4))
         shared("e", 0, 0, 256, 160)
-        shared("e", 0, 256, 256, 96)
+        shared("e", 0, 256, 256, 128)
         quantise("e", 0, 0, 256)
         multiply("e", 0, (0, 1))
-        shared("e", 1, 0, 256, 160)
+        shared("e", 1, 0, 128, 80)
+        shared("e", 1, 128, 128, 64)
+        quantise("e", 1, 0, 128)
+        multiply("e", 1, (0,))
         quantise("e", 0, 256, 256)
         multiply("e", 0, (2,))
-        quantise("e", 1, 0, 256)
-        multiply("e", 1, (0, 1))
-        multiply("e", 0, (3,))
+        quantise("e", 1, 128, 128)
+        multiply("e", 1, (1,))
         interleave("scalar", "e", 1, 256, 128)
         shared("e", 1, 384, 128, 80)
         quantise("e", 1, 256, 128)
         multiply("e", 1, (2,))
+        multiply("e", 0, (3,))
+        copy_out(0, CUT)
         quantise("e", 1, 384, 128)
         multiply("e", 1, (3,))
-        finish(0, 0, 512, nc.sync)
-        for m in (1, 2):
-            copy_out(m, CUT)
+        for m in range(3):
             finish_shared(m, CUT)
-        finish(3, 0, 512, nc.sync)
+            copy_out(m + 1, CUT)
+        finish_shared(3, CUT)

@@ -16,7 +16,6 @@ PACK = 4
 K_PASS = P * PACK
 T_TILE = 128
 RUN = 4
-CUT = 384
 
 FLOPS = 2 * (K + L) * D * T
 
@@ -36,7 +35,7 @@ def tile_mix_aux_tm_res_kernel(tc, w, dy, v, e, r, out):
             planes[name] = keep.tile([P, 2, 512], U8, name="plane_%s" % name, align_bytes=256)
             grouped[name] = keep.tile([P, 2, 512, PACK], BF16, name="grouped_%s" % name, align_bytes=256)
         sums = [psum.tile([T_TILE, D], F32, name="sum_%d" % m) for m in range(T // T_TILE)]
-        raws, wholes, residuals, plains, seen = {}, {}, {}, {}, {}
+        raws, wholes, residuals, seen = {}, {}, {}, {}
 
         def load(name, c, first, width, queue=nc.sync):
             raw = keep.tile([P, PACK, width], F32, name="raw_%s%d_%d" % (name, c, first), align_bytes=256)
@@ -106,18 +105,6 @@ def tile_mix_aux_tm_res_kernel(tc, w, dy, v, e, r, out):
                     stop=n == 3,
                 )
 
-        def copy_out(m, cut):
-            plain = keep.tile([P, D - cut], F32, name="plain_%d" % m, align_bytes=256)
-            nc.scalar.copy(out=plain[:], in_=sums[m][:, cut:])
-            plains[m] = plain
-
-        def finish_shared(m, cut):
-            result = keep.tile([P, D], F32, name="result_%d" % m, align_bytes=256)
-            residual = residuals[m, 0]
-            nc.gpsimd.tensor_tensor(out=result[:, cut:], in0=plains[m][:], in1=residual[:, cut:], op=mybir.AluOpType.add)
-            nc.vector.tensor_tensor(out=result[:, :cut], in0=sums[m][:, :cut], in1=residual[:, :cut], op=mybir.AluOpType.add)
-            nc.sync.dma_start(out=out[m * T_TILE : (m + 1) * T_TILE, :], in_=result[:])
-
         def finish(m, first, width, queue, loaded_at=0):
             result = keep.tile([P, width], F32, name="result_%d_%d" % (m, first), align_bytes=256)
             cols = slice(first, first + width)
@@ -162,14 +149,11 @@ def tile_mix_aux_tm_res_kernel(tc, w, dy, v, e, r, out):
         quantise("e", 1, 128, 128)
         multiply("e", 1, (1,))
         interleave("scalar", "e", 1, 256, 128)
-        shared("e", 1, 384, 128, 80)
+        shared("e", 1, 384, 128, 64)
         quantise("e", 1, 256, 128)
         multiply("e", 1, (2,))
         multiply("e", 0, (3,))
-        copy_out(0, CUT)
         quantise("e", 1, 384, 128)
         multiply("e", 1, (3,))
-        for m in range(3):
-            finish_shared(m, CUT)
-            copy_out(m + 1, CUT)
-        finish_shared(3, CUT)
+        for m in range(4):
+            finish(m, 0, D, nc.sync)

@@ -16,6 +16,8 @@ PACK = 4
 K_PASS = P * PACK
 T_TILE = 128
 RUN = 4
+BOTH = (0, 1)
+ALIGN = 256
 
 FLOPS = 2 * (K + L) * D * T
 
@@ -31,70 +33,55 @@ def tile_mix_aux_tm_res_kernel(tc, w, dy, v, e, r, out):
         partner = {"dy": "w", "e": "v"}
         codes, planes, grouped = {}, {}, {}
         for name in operands:
-            codes[name] = keep.tile([P, 2, 512], U32, name="codes_%s" % name, align_bytes=256)
-            planes[name] = keep.tile([P, 2, 512], U8, name="plane_%s" % name, align_bytes=256)
-            grouped[name] = keep.tile([P, 2, 512, PACK], BF16, name="grouped_%s" % name, align_bytes=256)
+            codes[name] = keep.tile([P, 2, 512], U32, name="codes_%s" % name, align_bytes=ALIGN)
+            planes[name] = keep.tile([P, 2, 512], U8, name="plane_%s" % name, align_bytes=ALIGN)
+            grouped[name] = keep.tile([P, 2, 512, PACK], BF16, name="grouped_%s" % name, align_bytes=ALIGN)
         sums = [psum.tile([T_TILE, D], F32, name="sum_%d" % m) for m in range(T // T_TILE)]
-        raws, wholes, residuals, seen = {}, {}, {}, {}
+        pieces, residuals, results, passes_done = [], {}, {}, {}
 
-        def load(name, c, first, width, queue=nc.sync):
-            raw = keep.tile([P, PACK, width], F32, name="raw_%s%d_%d" % (name, c, first), align_bytes=256)
-            rows = operands[name][0][c * K_PASS : (c + 1) * K_PASS, first : first + width]
-            queue.dma_start(out=raw[:], in_=rows.rearrange("(p j) x -> p j x", j=PACK))
-            raws[name, c, first] = raw[:]
+        def span(passes):
+            return slice(0, 2) if passes == BOTH else slice(passes, passes + 1)
 
-        def load_both(name):
-            raw = keep.tile([P, 2, PACK * 512], F32, name="raw_%s" % name, align_bytes=256)
-            nc.sync.dma_start(out=raw[:], in_=operands[name][0].rearrange("(c p j) x -> p c (j x)", j=PACK, p=P))
-            wholes[name] = raw
+        def load(name, passes, first, width, queue=nc.sync):
+            c = span(passes)
+            count = c.stop - c.start
+            raw = keep.tile([P, count, PACK, width], F32, name="raw_%d" % len(pieces), align_bytes=ALIGN)
+            rows = operands[name][0][c.start * K_PASS : c.stop * K_PASS, first : first + width]
+            queue.dma_start(out=raw[:], in_=rows.rearrange("(c p j) x -> p c j x", p=P, j=PACK))
+            pieces.append((name, c, first, width, raw))
 
-        def shared_both(name, on_vector):
-            source = wholes[name][:].rearrange("p c (j x i) -> p c x j i", j=PACK, i=RUN)
-            target = grouped[name][:].rearrange("p c (x i) j -> p c x j i", i=RUN)
-            cut = on_vector // RUN
-            nc.vector.tensor_copy(out=target[:, :, :cut], in_=source[:, :, :cut])
-            nc.scalar.copy(out=target[:, :, cut:], in_=source[:, :, cut:])
-
-        def quantise_both(name):
-            nc.vector.quantize_mx(
-                out=codes[name][:].rearrange("p c x -> p (c x)").bitcast(operands[name][1]),
-                scales=planes[name][:].rearrange("p c x -> p (c x)"),
-                in_=grouped[name][:].rearrange("p c x j -> p (c x j)"),
-            )
-
-        def load_residual(m, tiles, first=0, width=D):
-            residual = keep.tile([P, tiles, width], F32, name="residual_%d_%d" % (m, first), align_bytes=256)
-            rows = r[m * T_TILE : (m + tiles) * T_TILE, first : first + width]
-            nc.sync.dma_start(out=residual[:], in_=rows.rearrange("(m p) x -> p m x", p=P))
-            for i in range(tiles):
-                residuals[m + i, first] = residual[:, i, :]
-
-        def interleave(engine, name, c, first, width):
-            base = max(start for key, part, start in raws if (key, part) == (name, c) and start <= first)
-            source = raws[name, c, base][:, :, first - base : first - base + width].rearrange("p j (x i) -> p x j i", i=RUN)
-            target = grouped[name][:, c, first : first + width, :].rearrange("p (x i) j -> p x j i", i=RUN)
+        def copy(engine, name, passes, first, width):
+            c = span(passes)
+            held, base, raw = [
+                (held, base, raw)
+                for key, held, base, size, raw in pieces
+                if key == name and held.start <= c.start < held.stop and base <= first < base + size
+            ][0]
+            source = raw[:, c.start - held.start : c.stop - held.start, :, first - base : first - base + width]
+            source = source.rearrange("p c j (x i) -> p c x j i", i=RUN)
+            target = grouped[name][:, c, first : first + width, :].rearrange("p c (x i) j -> p c x j i", i=RUN)
             if engine == "vector":
                 nc.vector.tensor_copy(out=target, in_=source)
             else:
                 nc.scalar.copy(out=target, in_=source)
 
-        def shared(name, c, first, width, on_vector):
-            interleave("vector", name, c, first, on_vector)
-            interleave("scalar", name, c, first + on_vector, width - on_vector)
+        def shared(name, passes, first, width, on_vector):
+            copy("vector", name, passes, first, on_vector)
+            copy("scalar", name, passes, first + on_vector, width - on_vector)
 
-        def quantise(name, c, first, width):
-            cols = slice(first, first + width)
+        def quantise(name, passes, first, width):
+            c, cols = span(passes), slice(first, first + width)
             nc.vector.quantize_mx(
-                out=codes[name][:, c, cols].bitcast(operands[name][1]),
-                scales=planes[name][:, c, cols],
-                in_=grouped[name][:, c, cols, :].rearrange("p x j -> p (x j)"),
+                out=codes[name][:, c, cols].rearrange("p c x -> p (c x)").bitcast(operands[name][1]),
+                scales=planes[name][:, c, cols].rearrange("p c x -> p (c x)"),
+                in_=grouped[name][:, c, cols, :].rearrange("p c x j -> p (c x j)"),
             )
 
         def multiply(name, c, tiles):
             for m in tiles:
                 t_cols = slice(m * T_TILE, (m + 1) * T_TILE)
-                n = seen.get(m, 0)
-                seen[m] = n + 1
+                n = passes_done.get(m, 0)
+                passes_done[m] = n + 1
                 nc.tensor.matmul_mx(
                     out=sums[m][:],
                     lhsT=codes[name][:, c, t_cols].bitcast(operands[name][1]),
@@ -105,27 +92,30 @@ def tile_mix_aux_tm_res_kernel(tc, w, dy, v, e, r, out):
                     stop=n == 3,
                 )
 
-        def finish(m, first, width, queue, loaded_at=0):
-            result = keep.tile([P, width], F32, name="result_%d_%d" % (m, first), align_bytes=256)
-            cols = slice(first, first + width)
-            residual = residuals[m, loaded_at][:, first - loaded_at : first - loaded_at + width]
-            nc.vector.tensor_tensor(out=result[:], in0=sums[m][:, cols], in1=residual, op=mybir.AluOpType.add)
-            queue.dma_start(out=out[m * T_TILE : (m + 1) * T_TILE, cols], in_=result[:])
+        def load_residual(m, queue=nc.sync):
+            residuals[m] = keep.tile([P, D], F32, name="residual_%d" % m, align_bytes=ALIGN)
+            queue.dma_start(out=residuals[m][:], in_=r[m * T_TILE : (m + 1) * T_TILE, :])
 
-        load_both("w")
-        load_both("v")
-        for c in range(2):
-            load("dy", c, 0, 512)
+        def add(m):
+            results[m] = keep.tile([P, D], F32, name="result_%d" % m, align_bytes=ALIGN)
+            nc.vector.tensor_tensor(out=results[m][:], in0=sums[m][:], in1=residuals[m][:], op=mybir.AluOpType.add)
+
+        def store(m, queue=nc.sync):
+            queue.dma_start(out=out[m * T_TILE : (m + 1) * T_TILE, :], in_=results[m][:])
+
+        load("w", BOTH, 0, 512)
+        load("v", BOTH, 0, 512)
+        load("dy", 0, 0, 512)
+        load("dy", 1, 0, 512)
         load("e", 0, 0, 512)
         load("e", 1, 0, 256)
         load("e", 1, 256, 128)
         load("e", 1, 384, 128)
         for m in range(4):
-            load_residual(m, 1)
-
-        shared_both("w", 320)
-        quantise_both("w")
-        shared_both("v", 320)
+            load_residual(m)
+        shared("w", BOTH, 0, 512, 320)
+        quantise("w", BOTH, 0, 512)
+        shared("v", BOTH, 0, 512, 320)
         quantise("v", 0, 0, 512)
         for half in range(2):
             shared("dy", 0, 256 * half, 256, 160)
@@ -148,7 +138,7 @@ def tile_mix_aux_tm_res_kernel(tc, w, dy, v, e, r, out):
         multiply("e", 0, (2,))
         quantise("e", 1, 128, 128)
         multiply("e", 1, (1,))
-        interleave("scalar", "e", 1, 256, 128)
+        copy("scalar", "e", 1, 256, 128)
         shared("e", 1, 384, 128, 64)
         quantise("e", 1, 256, 128)
         multiply("e", 1, (2,))
@@ -156,4 +146,5 @@ def tile_mix_aux_tm_res_kernel(tc, w, dy, v, e, r, out):
         quantise("e", 1, 384, 128)
         multiply("e", 1, (3,))
         for m in range(4):
-            finish(m, 0, D, nc.sync)
+            add(m)
+            store(m, nc.scalar)

from contextlib import ExitStack

import concourse.mybir as mybir

K, L, D, T = 1024, 1024, 512, 512

F32 = mybir.dt.float32
BF16 = mybir.dt.bfloat16
U32 = mybir.dt.uint32
U8 = mybir.dt.uint8
E4M3 = mybir.dt.float8_e4m3fn_x4
E5M2 = mybir.dt.float8_e5m2_x4

P = 128
PACK = 4
K_PASS = P * PACK
T_TILE = 128
RUN = 4
BOTH = (0, 1)
ALIGN = 256

FLOPS = 2 * (K + L) * D * T


def tile_mix_aux_tm_res_kernel(tc, w, dy, v, e, r, out):
    nc = tc.nc
    with ExitStack() as ctx:
        keep = ctx.enter_context(tc.tile_pool(name="keep", bufs=1))
        psum = ctx.enter_context(tc.psum_pool(name="psum", bufs=1))
        ctx.enter_context(tc.manual_schedule())

        operands = {"w": (w, E4M3), "dy": (dy, E5M2), "v": (v, E4M3), "e": (e, E4M3)}
        partner = {"dy": "w", "e": "v"}
        codes, planes, grouped = {}, {}, {}
        for name in operands:
            codes[name] = keep.tile([P, 2, 512], U32, name="codes_%s" % name, align_bytes=ALIGN)
            planes[name] = keep.tile([P, 2, 512], U8, name="plane_%s" % name, align_bytes=ALIGN)
            grouped[name] = keep.tile([P, 2, 512, PACK], BF16, name="grouped_%s" % name, align_bytes=ALIGN)
        sums = [psum.tile([T_TILE, D], F32, name="sum_%d" % m) for m in range(T // T_TILE)]
        pieces, residuals, results, passes_done = [], {}, {}, {}

        def span(passes):
            return slice(0, 2) if passes == BOTH else slice(passes, passes + 1)

        def load(name, passes, first, width, queue=nc.sync):
            c = span(passes)
            count = c.stop - c.start
            raw = keep.tile([P, count, PACK, width], F32, name="raw_%d" % len(pieces), align_bytes=ALIGN)
            rows = operands[name][0][c.start * K_PASS : c.stop * K_PASS, first : first + width]
            queue.dma_start(out=raw[:], in_=rows.rearrange("(c p j) x -> p c j x", p=P, j=PACK))
            pieces.append((name, c, first, width, raw))

        def copy(engine, name, passes, first, width):
            c = span(passes)
            held, base, raw = [
                (held, base, raw)
                for key, held, base, size, raw in pieces
                if key == name and held.start <= c.start < held.stop and base <= first < base + size
            ][0]
            source = raw[:, c.start - held.start : c.stop - held.start, :, first - base : first - base + width]
            source = source.rearrange("p c j (x i) -> p c x j i", i=RUN)
            target = grouped[name][:, c, first : first + width, :].rearrange("p c (x i) j -> p c x j i", i=RUN)
            if engine == "vector":
                nc.vector.tensor_copy(out=target, in_=source)
            else:
                nc.scalar.copy(out=target, in_=source)

        def shared(name, passes, first, width, on_vector):
            copy("vector", name, passes, first, on_vector)
            copy("scalar", name, passes, first + on_vector, width - on_vector)

        def quantise(name, passes, first, width):
            c, cols = span(passes), slice(first, first + width)
            nc.vector.quantize_mx(
                out=codes[name][:, c, cols].rearrange("p c x -> p (c x)").bitcast(operands[name][1]),
                scales=planes[name][:, c, cols].rearrange("p c x -> p (c x)"),
                in_=grouped[name][:, c, cols, :].rearrange("p c x j -> p (c x j)"),
            )

        def multiply(name, c, tiles):
            for m in tiles:
                t_cols = slice(m * T_TILE, (m + 1) * T_TILE)
                n = passes_done.get(m, 0)
                passes_done[m] = n + 1
                nc.tensor.matmul_mx(
                    out=sums[m][:],
                    lhsT=codes[name][:, c, t_cols].bitcast(operands[name][1]),
                    lhsT_scale=planes[name][:, c, t_cols],
                    rhs=codes[partner[name]][:, c, :].bitcast(E4M3),
                    rhs_scale=planes[partner[name]][:, c, :],
                    start=n == 0,
                    stop=n == 3,
                )

        def load_residual(m, queue=nc.sync):
            residuals[m] = keep.tile([P, D], F32, name="residual_%d" % m, align_bytes=ALIGN)
            queue.dma_start(out=residuals[m][:], in_=r[m * T_TILE : (m + 1) * T_TILE, :])

        def add(m):
            results[m] = keep.tile([P, D], F32, name="result_%d" % m, align_bytes=ALIGN)
            nc.vector.tensor_tensor(out=results[m][:], in0=sums[m][:], in1=residuals[m][:], op=mybir.AluOpType.add)

        def store(m, queue=nc.sync):
            queue.dma_start(out=out[m * T_TILE : (m + 1) * T_TILE, :], in_=results[m][:])

        load("w", BOTH, 0, 512)
        load("v", BOTH, 0, 512)
        load("dy", 0, 0, 512)
        load("dy", 1, 0, 512)
        load("e", 0, 0, 512)
        load("e", 1, 0, 256)
        load("e", 1, 256, 128)
        load("e", 1, 384, 128)
        for m in range(4):
            load_residual(m)
        shared("w", BOTH, 0, 512, 320)
        quantise("w", BOTH, 0, 512)
        shared("v", BOTH, 0, 512, 320)
        quantise("v", 0, 0, 512)
        for half in range(2):
            shared("dy", 0, 256 * half, 256, 160)
        for half in range(2):
            quantise("dy", 0, 256 * half, 256)
            multiply("dy", 0, (2 * half, 2 * half + 1))
        quantise("v", 1, 0, 512)
        shared("dy", 1, 0, 512, 320)
        quantise("dy", 1, 0, 512)
        multiply("dy", 1, range(4))
        shared("e", 0, 0, 256, 160)
        shared("e", 0, 256, 256, 128)
        quantise("e", 0, 0, 256)
        multiply("e", 0, (0, 1))
        shared("e", 1, 0, 128, 80)
        shared("e", 1, 128, 128, 64)
        quantise("e", 1, 0, 128)
        multiply("e", 1, (0,))
        quantise("e", 0, 256, 256)
        multiply("e", 0, (2,))
        quantise("e", 1, 128, 128)
        multiply("e", 1, (1,))
        copy("scalar", "e", 1, 256, 128)
        shared("e", 1, 384, 128, 64)
        quantise("e", 1, 256, 128)
        multiply("e", 1, (2,))
        multiply("e", 0, (3,))
        quantise("e", 1, 384, 128)
        multiply("e", 1, (3,))
        for m in range(4):
            add(m)
            store(m, nc.scalar)
